import numpy as np, ml_dtypes
CORES = [2,3,6,7,58,59,62,63,114,115,118,119]
N = 12
import mx_ref
BF = ml_dtypes.bfloat16
def entries(a):
    return np.ascontiguousarray(a.T).reshape(-1)
def table(e):
    return np.ascontiguousarray(np.reshape(e, (-1, 16)).T).astype(np.int32)
def cols(t, e):
    v = np.concatenate([t.reshape(128, -1, 4), np.zeros((128, 1, 4), BF)], axis=1)
    return np.ascontiguousarray(v[:, e]).reshape(128, -1)
def f(rng, *shape):
    return mx_ref.flush((rng.standard_normal(shape, dtype=np.float32) * np.exp2(rng.integers(-2, 3, shape[:-1] + (1,)))).astype(BF))
def wide(rng, *shape, cols=0):
    v = rng.standard_normal(shape, dtype=np.float32) * np.exp2(rng.integers(-12, 13, shape)).astype(np.float32)
    if cols: v *= np.repeat(np.exp2(rng.integers(-cols, cols + 1, shape[:-2] + (1, shape[-1] // 4))) * (rng.random(shape[:-2] + (1, shape[-1] // 4)) > 0.0625), 4, axis=-1).astype(np.float32)
    return mx_ref.flush(v.astype(BF))
T, S, CAPP = 512, 256, 32
def lists(rng, most=None, own=False, share=False, edge=False):
    o, c, m = [], [], []
    for r in range(N):
        n = np.zeros(N, int)
        if own: n[r] = CAPP
        if most is not None:
            for q in rng.permutation(N)[:most]: n[q] = CAPP
            n = np.minimum(n, np.maximum(0, S - (np.cumsum(n) - n)))
        while n.sum() < S:
            q = rng.integers(0, N)
            if n[q] < CAPP: n[q] += 1
        slots = np.full(N * CAPP, -1); used = []
        for q in range(N):
            k = q * CAPP + rng.permutation(CAPP)[:n[q]]; used += list(k)
            slots[k] = rng.integers(0, T) if share else rng.choice([0, T - 1], n[q]) if edge else rng.integers(0, T, n[q])
        o.append(table(rng.choice([0, T - 1], S) if edge else rng.integers(0, T, S))); c.append(table(slots)); m.append(table(rng.permutation(used)))
    return {"own": np.stack(o), "want": np.stack(c), "slot": np.stack(m)}
def setup_inputs(rng):
    return {"x": f(rng, N, 128, 4 * T), "w": f(rng, N, 128, 512), **lists(rng)}
def setup_inputs_edge(rng):
    return {**setup_inputs(rng), **lists(rng, edge=True)}
def setup_inputs_full(rng):
    return {**setup_inputs(rng), **lists(rng, most=S // CAPP)}
def setup_inputs_self(rng):
    return {**setup_inputs(rng), **lists(rng, own=True)}
def setup_inputs_share(rng):
    return {**setup_inputs(rng), **lists(rng, share=True)}
def setup_inputs_spread(rng):
    d = setup_inputs(rng); d["x"] = wide(rng, N, 128, 4 * T, cols=8); return d
def check_inputs(d):
    b = []
    for r in range(N):
        o, c, m = entries(d["own"][r]), entries(d["want"][r]), entries(d["slot"][r])
        if o.min() < 0 or o.max() >= T: b.append("own")
        if c.min() < -1 or c.max() >= T: b.append("want")
        if m.min() < 0 or m.max() >= N * CAPP or len(set(m.tolist())) != S or (c[m] < 0).any() or (c >= 0).sum() != S: b.append("slot")
    return b
def decode(q):
    out = np.zeros(q[0].shape, np.float32)
    for b in range(4):
        e = np.zeros((128, 128, 4), np.float32); e[np.arange(128), np.arange(128), b] = 1
        out[:, b::4] = mx_ref.matmul(mx_ref.quantize(e.reshape(128, 512).astype(BF)), q)
    return out
def reference(x, w, own, want, slot):
    M = []
    for r in range(N):
        c = entries(want[r])
        arrived = np.concatenate([decode(mx_ref.quantize(cols(x[q], c[q * CAPP:(q + 1) * CAPP]))) for q in range(N)], axis=1)
        far = arrived.reshape(128, -1, 4)[:, entries(slot[r])].reshape(128, -1)
        M.append(mx_ref.quantize(((cols(x[r], entries(own[r])).astype(np.float32) + far) * np.float32(0.5)).astype(BF)))
    y = np.zeros((N, 128, 3 * S), np.float32)
    for r in range(N):
        for i in range(3): y[r][:, S * i:S * i + S] = mx_ref.matmul(mx_ref.quantize(w[r]), M[(r - 1 + i) % N])
    return {"y": y}

import numpy as np
from concourse.bass import DstId, RemoteDMATransfer
from concourse.mybir import dt, AluOpType, ActivationFunctionType

F8, U8, F32, BF, I32, U16 = "float8_e4m3fn_x4", "uint8", "float32", "bfloat16", "int32", "uint16"
SCRATCH = {
    "lsend": ("dram", [192, 2], I32),
    "lland": ("dram", [12, 128, 2], I32),
    "xs": ("sbuf", [128, 2048], BF),
    "ws": ("sbuf", [128, 512], BF),
    "wc": ("sbuf", [128, 128], F8), "wp": ("sbuf", [128, 128], U8),
    "ones": ("sbuf", [128, 516], BF), "band": ("sbuf", [128, 516], BF),
    "ec": ("sbuf", [128, 512], F8), "ep": ("sbuf", [128, 512], U8),
    "raw": ("sbuf", [16, 32], I32),
    "i1": ("sbuf", [16, 16], I32), "i2": ("sbuf", [16, 16], I32), "i3": ("sbuf", [16, 16], I32),
    "i4": ("sbuf", [16, 16], I32), "i5": ("sbuf", [16, 16], I32), "i6": ("sbuf", [16, 16], I32), "i7": ("sbuf", [16, 16], I32),
    "oo": ("sbuf", [128, 32], U16),
    "lf": ("sbuf", [128, 32], I32), "ff": ("sbuf", [128, 64], F32), "tf": ("sbuf", [128, 64], F32), "of": ("sbuf", [128, 16], U16),
    "ln": ("sbuf", [128, 32], I32), "fn": ("sbuf", [128, 64], F32), "tn": ("sbuf", [128, 64], F32), "on": ("sbuf", [128, 8], U16),
    "h": ("sbuf", [128, 1536], BF),
    "cq": ("sbuf", [128, 384], F8), "sq": ("sbuf", [128, 384], U8),
    "cf": ("sbuf", [128, 384], F8), "sf": ("sbuf", [128, 384], U8),
    "f": ("sbuf", [128, 1536], F32),
    "ow": ("sbuf", [128, 1024], BF),
    "m": ("sbuf", [128, 1024], BF),
    "mc": ("sbuf", [128, 256], F8), "mp": ("sbuf", [128, 256], U8),
    "lc": ("sbuf", [128, 256], F8), "lp": ("sbuf", [128, 256], U8),
    "rc": ("sbuf", [128, 256], F8), "rp": ("sbuf", [128, 256], U8),
    "ys": ("sbuf", [128, 768], F32),
    "pa": ("psum", [128, 2048], F32), "pb": ("psum", [128, 2048], F32),
}
SEMAPHORES = ["wnt", "self", "xld", "wld", "old", "rep", "lfl", "lnl", "slf", "yst",
              "lfa", "lna", "sent", "c0", "c1", "c2", "nl", "nr",
              "ones", "zf", "zn", "band", "eq", "wq", "d1", "d2", "d3", "d4", "d5", "ofs",
              "fc", "ft", "fo", "nc", "nt", "no", "g0", "g1", "g2", "q0", "q1", "q2", "ow",
              "p1", "p2", "ga", "mq", "mo", "ml", "mr", "co", "cl", "cr"] \
             + ["m%d_%d" % (k, b) for k in range(3) for b in range(4)] + ["k%d" % b for b in range(4)]
CAPP, S, XC = 32, 256, 512


def rank_program(g, core, T, topo):
    rank = T.rank_of(core)
    if rank is None:
        return
    cores, n = list(T.cores), len(T.cores)
    chips = []
    for c in cores:
        if topo.chip(c) not in chips:
            chips.append(topo.chip(c))
    nc = len(chips)
    members = [[c for c in cores if topo.chip(c) == ch] for ch in chips]
    me = chips.index(topo.chip(core))
    loc = members[me].index(core)
    per = len(members[me])
    order = [members[(me + 1) % nc], members[(me + 2) % nc], members[me]]
    V, A, Y, P = g.vector, g.scalar, g.sync, g.tensor
    mx, mult, add, sub = AluOpType.max, AluOpType.mult, AluOpType.add, AluOpType.subtract
    tot, sem = {}, T.sem

    def up(call, name, k=1):
        call.then_inc(sem[name], k)
        tot[name] = tot.get(name, 0) + k

    def wait(queue, *names):
        for s in names:
            queue.wait_ge(sem[s], tot[s])

    def bits(engines):
        return sum(1 << e for e in engines)

    def dst(c):
        rid, pid, _ = topo.addr(c)
        return DstId(rid=rid, pnc=pid)

    def send(transfers):
        g.remote_dma_fused([RemoteDMATransfer(dst_ids=[dst(c) for c in cs], dma_engine_mask=bits(en), remote_sem=sem[rs], srcs=[src], dsts=list(ds))
                            for src, ds, cs, en, rs in transfers], local_sem=sem["sent"])
        tot["sent"] = tot.get("sent", 0) + sum(len(t[3]) for t in transfers)

    off_e = list(topo.engines(core, order[0][0]))
    all_e = list(topo.engines(core, [c for c in members[me] if c != core][0]))
    in_e = [e for e in all_e if e not in off_e]

    for k in range(n):
        q = cores.index(order[k // per][k % per])
        up((Y if k % 2 == 0 else A).dma_start(T.lsend[16 * k:16 * k + 16, :], T.want[:, 2 * q:2 * q + 2]), "wnt", 16)
    up(Y.dma_start(T.raw[:, 0:16], T.own[:]), "old", 16)
    up(A.dma_start(T.raw[:, 16:32], T.slot[:]), "old", 16)
    up(Y.dma_start(T.xs[:], T.x[:]), "xld", 16)
    up(A.dma_start(T.ws[:], T.w[:]), "wld", 16)
    up(Y.dma_start(T.lland[2 * per + loc, 64 + 16 * loc:80 + 16 * loc, :], T.want[:, 2 * rank:2 * rank + 2]), "self", 16)

    up(V.memset(T.ones[:], 1.0), "ones")
    up(V.memset(T.lf[:], 0), "zf")
    up(V.memset(T.ln[:], 0), "zn")
    wait(g, "ones")
    up(g.affine_select(T.band[:], T.ones[:], [[1, 516]], AluOpType.is_equal, 0.0, -3, -4), "band")

    wait(g, "wnt")
    one, two = T.lsend[0:128, :], T.lsend[64:192, :]
    send([(one, [T.lland[per + loc]] * per, order[0], off_e[0:1], "lfa"),
          (two, [T.lland[loc]] * per, order[1], off_e[1:2], "lfa")])
    peers = [c for c in members[me] if c != core]
    send([(two, [T.lland[2 * per + loc]] * len(peers), peers, all_e, "lna")])
    tot["lfa"] = 2 * per
    tot["lna"] = len(peers) * len(all_e)

    wait(V, "band")
    for b in range(4):
        up(V.quantize_mx(T.ec[:, 128 * b:128 * b + 128], T.ep[:, 128 * b:128 * b + 128], T.band[:, 3 - b:515 - b]), "eq")
    wait(V, "old")
    own, slot = T.raw[:, 0:16], T.raw[:, 16:32]
    up(V.tensor_scalar(T.oo[0:16, 0:16], own, 4, None, mult), "ofs")
    up(V.tensor_scalar(T.i1[:], slot, 15, None, AluOpType.bitwise_and), "d1")
    up(V.tensor_scalar(T.i2[:], slot, 4, 1, AluOpType.logical_shift_right, AluOpType.bitwise_and), "d1")
    wait(V, "d1")
    up(V.tensor_tensor(T.i3[:], slot, T.i1[:], add), "d2")
    up(V.tensor_scalar(T.i4[:], T.i2[:], -15, None, mult), "d2")
    wait(V, "d2")
    up(V.tensor_tensor(T.i5[:], T.i3[:], T.i4[:], add), "d3")
    wait(V, "d3")
    turn = CAPP * per * ((me + 1) % nc)
    up(V.tensor_scalar(T.i6[:], T.i5[:], turn, CAPP * n, AluOpType.is_lt, mult), "d4")
    wait(V, "d4")
    up(V.tensor_tensor(T.i7[:], T.i5[:], T.i6[:], add), "d5")
    wait(V, "d5")
    up(V.tensor_scalar(T.oo[0:16, 16:32], T.i7[:], turn, None, sub), "ofs")
    wait(V, "wld")
    up(V.quantize_mx(T.wc[:], T.wp[:], T.ws[:]), "wq")

    wait(Y, "ofs")
    for k in range(1, 8):
        up(Y.dma_start(T.oo[16 * k:16 * k + 16, :], T.oo[0:16, :]), "rep", 16)

    for q, blocks in ((A, (0, 1)), (Y, (2, 3))):
        wait(q, "zf", "lfa")
        for a in blocks:
            up(q.dma_start(T.lf[32 * a:32 * a + 2 * per, :], T.lland[0:2 * per, 16 * loc:16 * loc + 16, :]), "lfl", 16)
    wait(Y, "zn", "self", "lna")
    for a in range(4):
        up(Y.dma_start(T.ln[32 * a:32 * a + per, :], T.lland[2 * per:3 * per, 64 + 16 * loc:80 + 16 * loc, :]), "lnl", 16)

    def lists(raw, wide, turned, off, k, loaded, s1, s2, s3):
        wait(V, loaded)
        for j in range(4):
            up(V.tensor_scalar(wide[:, 16 * j:16 * j + 16], raw[:, 16 * (j // 2):16 * (j // 2) + 16], 0, 4, mx, mult), s1)
        wait(V, s1)
        up(V.transpose(turned[:], wide[:]), s2)
        wait(V, s2)
        for t in range(2):
            up(V.tensor_copy(off[:, t:2 * k:2], turned[:, 32 * t:32 * t + k]), s3)

    def gather(k, off, j):
        for t in range(4):
            out, win = T.h[:, 512 * k + t:512 * k + 512:4], T.xs[:, t:4 * XC].indirect(off[:, j:j + 8])
            if t < 2:
                up(V.tensor_copy(out, win), "g%d" % k)
            else:
                up(A.activation(out, win, ActivationFunctionType.Copy), "g%d" % k)
        wait(V, "g%d" % k)
        up(V.quantize_mx(T.cq[:, 128 * k:128 * k + 128], T.sq[:, 128 * k:128 * k + 128], T.h[:, 512 * k:512 * k + 512]), "q%d" % k)

    lists(T.lf, T.ff, T.tf, T.of, 2 * per, "lfl", "fc", "ft", "fo")
    wait(A, "xld", "fo")
    wait(V, "xld", "fo")
    for k in range(2):
        gather(k, T.of, 8 * k)
    lists(T.ln, T.fn, T.tn, T.on, per, "lnl", "nc", "nt", "no")
    wait(A, "no")
    wait(V, "no")
    gather(2, T.on, 0)

    half = len(in_e) // 2
    near_e = [in_e[:half], in_e[half:half + half // 2], in_e[half + half // 2:]]
    w = len(off_e) // per
    for k in range(3):
        wait(g, "q%d" % k)
        to = [(j, c) for j, c in enumerate(order[k]) if c != core]
        eng = [off_e[w * i:w * i + w] for i in range(per)] if k < 2 else near_e
        place = CAPP * ((per, 0, 2 * per)[k] + loc)
        rs = ("c1", "c0", "c2")[k]
        for codes in (True, False):
            tr = []
            for i, (j, c) in enumerate(to):
                col = 128 * k + CAPP * j
                if codes:
                    s, d = T.cq[:, col:col + CAPP].bitcast(dt.uint8), T.cf[:, place:place + CAPP].bitcast(dt.uint8)
                else:
                    s, d = T.sq[:, col:col + CAPP], T.sf[:, place:place + CAPP]
                tr.append((s, [d], [c], eng[i], rs))
            send(tr)
    tot["c0"] = tot["c1"] = 2 * per * w
    tot["c2"] = sum(2 * len(near_e[[p for p in members[me] if p != c].index(core)]) for c in peers)
    wait(Y, "q2")
    mine = 2 * per * CAPP + CAPP * loc
    up(Y.dma_start(T.cf[:, mine:mine + CAPP].bitcast(dt.uint8), T.cq[:, mine:mine + CAPP].bitcast(dt.uint8)), "slf", 16)
    up(Y.dma_start(T.sf[:, mine:mine + CAPP], T.sq[:, mine:mine + CAPP]), "slf", 16)

    wait(V, "rep")
    wait(A, "rep")
    for b in range(4):
        out, win = T.ow[:, 256 * b:256 * b + 256], T.xs[:, b:4 * XC].indirect(T.oo[:, 0:16])
        if b < 2:
            up(V.tensor_scalar(out, win, 0.5, None, mult), "ow")
        else:
            up(A.activation(out, win, ActivationFunctionType.Copy, scale=0.5), "ow")

    wait(P, "eq")
    for k, ps in ((1, T.pa), (2, T.pb), (0, T.pa)):
        wait(P, "c%d" % k)
        if k == 2:
            wait(P, "slf")
        if k == 0:
            wait(P, "p1")
        for b in range(4):
            up(P.matmul_mx(ps[:, 512 * b:512 * b + 128], T.ec[:, 128 * b:128 * b + 128], T.ep[:, 128 * b:128 * b + 128],
                           T.cf[:, 128 * k:128 * k + 128], T.sf[:, 128 * k:128 * k + 128], True, True), "m%d_%d" % (k, b))
        for b in range(4):
            wait(A, "m%d_%d" % (k, b))
            up(A.activation(T.f[:, 384 * b + 128 * k:384 * b + 128 * k + 128], ps[:, 512 * b:512 * b + 128],
                            ActivationFunctionType.Copy, scale=0.5), "p%d" % k if k else "k%d" % b)

    wait(V, "p1", "p2", "ow")
    for b in range(4):
        wait(V, "k%d" % b)
        up(V.tensor_tensor(T.m[:, b:4 * S:4], T.f[:, 384 * b:384 * b + 384].indirect(T.oo[:, 16:32]), T.ow[:, 256 * b:256 * b + 256], add), "ga")
    wait(V, "ga")
    up(V.quantize_mx(T.mc[:], T.mp[:], T.m[:]), "mq")
    left, right = cores[(rank - 1) % n], cores[(rank + 1) % n]
    if topo.chip(left) != topo.chip(core):
        el, er = off_e, in_e
    else:
        el, er = in_e, off_e
    wait(g, "mq")
    send([(T.mc[:].bitcast(dt.uint8), [T.rc[:].bitcast(dt.uint8)], [left], el, "nr"),
          (T.mc[:].bitcast(dt.uint8), [T.lc[:].bitcast(dt.uint8)], [right], er, "nl")])
    send([(T.mp[:], [T.rp[:]], [left], el, "nr"), (T.mp[:], [T.lp[:]], [right], er, "nl")])
    tot["nl"] = tot["nr"] = 2 * len(off_e)

    def product(codes, plane, bank, s, arrived, i, copier, sc, storer):
        wait(P, *arrived)
        up(P.matmul_mx(T.pb[:, 512 * bank:512 * bank + S], T.wc[:], T.wp[:], codes[:], plane[:], True, True), s)
        wait(copier, s)
        out, src = T.ys[:, S * i:S * i + S], T.pb[:, 512 * bank:512 * bank + S]
        if copier is A:
            up(A.activation(out, src, ActivationFunctionType.Copy), sc)
        else:
            up(V.tensor_copy(out, src), sc)
        wait(storer, sc)
        up(storer.dma_start(T.y[:, S * i:S * i + S], out), "yst", 16)

    product(T.mc, T.mp, 0, "mo", ("wq", "mq", "p2"), 1, V, "co", Y)
    sides = [(T.lc, T.lp, 1, "ml", ("nl",), 0, V, "cl", Y), (T.rc, T.rp, 2, "mr", ("nr",), 2, A, "cr", A)]
    if topo.chip(left) != topo.chip(core):
        sides.reverse()
    for s in sides:
        product(*s)
    wait(Y, "yst")
    wait(g, "sent")
